import numpy as np
import ml_dtypes


def mxq(x, axis, fmt="e4m3"):
    dtype, down = {"e4m3": (ml_dtypes.float8_e4m3fn, 7), "e5m2": (ml_dtypes.float8_e5m2, 14)}[fmt]
    v = np.moveaxis(np.asarray(x, np.float32).astype(ml_dtypes.bfloat16).astype(np.float64), axis, -1)
    blocks = v.reshape(v.shape[:-1] + (-1, 32))
    amax = np.abs(blocks).max(-1, keepdims=True)
    byte = np.maximum(np.where(amax > 0, np.frexp(amax)[1] - 1 + 127, 0) - down, 1)
    scale = np.exp2(byte - 127.0)
    codes = (blocks / scale).astype(np.float32).astype(dtype).astype(np.float64)
    return np.moveaxis((codes * scale).reshape(v.shape), -1, axis)


WIDE = False


def mx_kscale(k):
    if not WIDE:
        return np.ones(k)
    levels = np.array([10, -10, 5, -5, 0])
    if k % 512:
        return np.exp2(np.random.permutation(np.resize(levels, k // 32))).repeat(32)
    a = np.empty((k // 512, 16))
    for p in range(k // 512):
        a[p, :8] = np.random.permutation(np.resize(levels, 8))
        for g in range(8):
            far = levels[np.abs(levels - a[p, g]) >= 10]
            a[p, g + 8] = far[np.random.randint(len(far))]
    return np.exp2(a.ravel()).repeat(32)


def f64(x):
    return np.asarray(x).astype(np.float64)


def striped(idx):
    return np.tile(np.asarray(idx).reshape(-1, 16).T, (8, 1)).astype(np.uint16)


def unstriped(offs):
    return offs[:16].T.reshape(-1).astype(np.int64)


E2M1 = np.array([0.0, 0.5, 1.0, 1.5, 2.0, 3.0, 4.0, 6.0, -0.0, -0.5, -1.0, -1.5, -2.0, -3.0, -4.0, -6.0])


def pack_weight(w, fmt):
    k, n = w.shape
    w = f64(np.asarray(w, np.float32).astype(ml_dtypes.bfloat16)).reshape(k // 32, 32, n)
    amax = np.abs(w).max(1)
    if fmt == "e4m3":
        byte = np.frexp(amax)[1] - 1 + 127 - 7
    else:
        mant, ex = np.frexp(amax / 6.0)
        byte = np.where(mant > 0.5, ex, ex - 1) + 127
    byte = np.clip(np.where(amax > 0, byte, 1), 1, 254)
    scaled = (w * np.exp2(127.0 - byte)[:, None, :]).reshape(k, n).astype(np.float32)
    by_word = np.ascontiguousarray(scaled.reshape(k // 512, 128, 4, n).transpose(0, 1, 3, 2))
    if fmt == "e4m3":
        words = by_word.astype(ml_dtypes.float8_e4m3fn).view(np.uint8)
    else:
        c = by_word.astype(ml_dtypes.float4_e2m1fn).view(np.uint8) & 0xF
        words = (c[..., 0::2] | (c[..., 1::2] << 4)).reshape(k // 512, 128, 2 * n)
    return np.ascontiguousarray(words), np.ascontiguousarray(byte.astype(np.uint8).reshape(k // 512, 16, n))


def unpack_weight(words, scales, fmt):
    g, _, n = scales.shape
    words = np.ascontiguousarray(words).reshape(g, 128, n, -1)
    if fmt == "e4m3":
        vals = words.view(ml_dtypes.float8_e4m3fn).astype(np.float64)
    else:
        nib = np.empty((g, 128, n, 4), np.uint8)
        nib[..., 0::2] = words & 0xF
        nib[..., 1::2] = words >> 4
        vals = E2M1[nib]
    vals = vals * np.repeat(np.exp2(scales.astype(np.float64) - 127.0), 8, axis=1)[..., None]
    return vals.transpose(0, 1, 3, 2).reshape(g * 512, n)


def bf(x):
    return np.asarray(x, np.float32).astype(ml_dtypes.bfloat16)


def planes(Y):
    r, m = Y.shape
    b = f64(bf(Y)).reshape(r // 32, 32, m)
    amax = np.abs(b).max(1)
    byte = np.clip(np.where(amax > 0, np.frexp(amax)[1] - 1 + 127 - 7, 1), 1, 254)
    codes = (b * np.exp2(127.0 - byte)[:, None, :]).reshape(r, m).astype(np.float32).astype(ml_dtypes.float8_e4m3fn).view(np.uint8)
    words = codes.reshape(r // 512, 128, 4, m).transpose(0, 1, 3, 2)
    return np.ascontiguousarray(words), np.ascontiguousarray(byte.astype(np.uint8).reshape(r // 512, 16, m))


K, T, J, I, N = 1024, 1024, 512, 512, 512


def setup_inputs():
    n = np.random.standard_normal
    idx = np.random.permutation(T)[:J]
    idx2 = np.random.permutation(T)[:I]
    fk = mx_kscale(K)
    xtp = pack_weight(n((K, T)) / fk[:, None], "e2m1")
    wbp = pack_weight(n((K, N)) * 1 / np.sqrt(K) * fk[:, None], "e4m3")
    return {
        "xt_words": xtp[0],
        "xt_scales": xtp[1],
        "wa": (n((K, N)) * 1 / np.sqrt(K) * fk[:, None]).astype(np.float32),
        "wb_words": wbp[0],
        "wb_scales": wbp[1],
        "gb": (np.random.uniform(0.4, 1.2, (1, I))).astype(np.float32),
        "res": (1.0 * n((N, T))).astype(np.float32),
        "offs": striped(idx),
        "offs2": striped(idx2),
    }


def reference(xt_words, xt_scales, wa, wb_words, wb_scales, gb, res, offs, offs2):
    idx = unstriped(offs)
    idx2 = unstriped(offs2)
    xtu = unpack_weight(xt_words, xt_scales, "e2m1")
    wbu = unpack_weight(wb_words, wb_scales, "e4m3")
    waq = mxq(f64(wa), 0, "e4m3")
    xtidxg = xtu[:, idx]
    p = waq.T @ xtidxg
    xtidx2g = xtu[:, idx2]
    q = wbu.T @ xtidx2g
    qw = q * f64(gb)
    pg = np.zeros((N, T))
    pg[:, idx] = p
    qg = np.zeros((N, T))
    qg[:, idx2] = qw
    y = pg + qg * np.exp(0.0 - np.abs(pg)) + 0.3 * f64(res)
    words, scales = planes(y)
    return y, words, scales

@@ -1,0 +1,210 @@
+from contextlib import ExitStack
+
+import concourse.mybir as mybir
+from concourse.masks import make_identity
+
+K, T, J, N = 1024, 1024, 512, 512
+FLOPS = 2 * 2 * K * N * J
+
+F32 = mybir.dt.float32
+BF16 = mybir.dt.bfloat16
+I32 = mybir.dt.int32
+U32 = mybir.dt.uint32
+U16 = mybir.dt.uint16
+U8 = mybir.dt.uint8
+FP8X4 = mybir.dt.float8_e4m3fn_x4
+FP4X4 = mybir.dt.float4_e2m1fn_x4
+ALU = mybir.AluOpType
+ACT = mybir.ActivationFunctionType
+
+P = 128
+PACK = 4
+PASSES = K // (P * PACK)
+QUADS = 4
+HALVES = 2
+CHUNKS = 4
+RES_WEIGHT = 0.3
+
+
+def tile_moe_second_choice_where_first_is_weak_pl_kernel(
+    tc, xt_words, xt_scales, wa, wb_words, wb_scales, gb, res, offs, offs2, out_0, out_1, out_2
+):
+    nc = tc.nc
+    with ExitStack() as ctx:
+        keep = ctx.enter_context(tc.tile_pool(name="keep", bufs=1))
+        ring = ctx.enter_context(tc.tile_pool(name="ring", bufs=2))
+        psum_qt = ctx.enter_context(tc.psum_pool(name="psum_qt", bufs=4))
+        psum = ctx.enter_context(tc.psum_pool(name="psum", bufs=2))
+
+        list_a = keep.tile([P, J // 16], U16, name="list_a")
+        list_b = keep.tile([P, J // 16], U16, name="list_b")
+        x_scale = keep.tile([P, T], U8, name="x_scale", align_bytes=64)
+        x_word = [keep.tile([P, 2 * T], U8, name=f"x_word{z}", align_bytes=64) for z in range(PASSES)]
+        nc.vector.memset(x_scale[:].bitcast(I32), 0)
+        nc.sync.dma_start(list_a[:], offs)
+        for z in range(PASSES):
+            nc.sync.dma_start(x_word[z][:].bitcast(I32), xt_words[z].bitcast(I32))
+        nc.sync.dma_start(list_b[:], offs2)
+        for q in range(QUADS):
+            nc.scalar.dma_start(
+                x_scale[32 * q : 32 * q + 8, :].bitcast(I32), xt_scales[:, 4 * q : 4 * q + 4, :].bitcast(I32)
+            )
+
+        hw = N // HALVES
+        wa_raw = {}
+        for z in range(PASSES):
+            rows = wa[z * 512 : (z + 1) * 512, :].rearrange("(p j) c -> p j c", j=PACK)
+            for h in range(HALVES):
+                wa_raw[z, h] = keep.tile([P, PACK, hw], F32, name=f"stage{HALVES * z + h}")
+                nc.sync.dma_start(wa_raw[z, h][:], rows[:, :, h * hw : (h + 1) * hw])
+
+        wb_word = keep.tile([P, PASSES, N], I32, name="wb_word", align_bytes=64)
+        wb_scale = keep.tile([P, PASSES, N], U8, name="wb_scale", align_bytes=64)
+        nc.gpsimd.memset(wb_scale[:].bitcast(I32), 0)
+        for q in range(QUADS):
+            nc.sync.dma_start(
+                wb_scale[32 * q : 32 * q + 4, :, :].bitcast(I32),
+                wb_scales[:, 4 * q : 4 * q + 4, :].rearrange("z r n -> r z n").bitcast(I32),
+            )
+        nc.sync.dma_start(wb_word[:], wb_words.rearrange("z p n t -> p z (n t)").bitcast(I32))
+        gate = keep.tile([P, PACK], F32, name="gate")
+        with nc.allow_non_contiguous_dma(reason="one gate value a partition"):
+            nc.sync.dma_start(gate[:], gb[0].rearrange("(s p) -> p s", p=P))
+        res_rows = res.rearrange("(p t) c -> p t c", t=PACK)
+        out_rows = out_0.rearrange("(p t) c -> p t c", t=PACK)
+
+        p_win = [keep.tile([P, T], F32, name=f"p_win{i}") for i in range(2)]
+        q_win = [keep.tile([P, T], F32, name=f"q_win{i}") for i in range(2)]
+        for w in (p_win[0], q_win[0], p_win[1], q_win[1]):
+            nc.vector.memset(w[:], 0.0)
+        ident = keep.tile([P, P], F32, name="ident")
+        make_identity(nc, ident[:])
+
+        g_scale0 = keep.tile([P, 2 * J], U8, name="g_scale0", align_bytes=64)
+        g_scale1 = keep.tile([P, 2 * J], U8, name="g_scale1", align_bytes=64)
+        nc.gpsimd.memset(g_scale1[:].bitcast(I32), 0)
+        g_scale = [g_scale0, g_scale1]
+        g_word = {}
+
+        def gather_words(name, lst):
+            for z in range(PASSES):
+                g_word[name, z] = keep.tile([P, 2 * J], U8, name=f"g_word_{name}{z}", align_bytes=64)
+                nc.vector.tensor_copy(g_word[name, z][:].bitcast(U16), x_word[z][:].bitcast(U16).indirect(lst[:]))
+
+        gather_words("a", list_a)
+        nc.vector.tensor_copy(g_scale0[:, 0:J], x_scale[:].indirect(list_a[:]))
+        nc.vector.tensor_copy(g_scale0[:, J : 2 * J], x_scale[:].indirect(list_b[:]))
+        nc.gpsimd.dma_start(g_scale1[0:112, :].bitcast(I32), g_scale0[4:116, :].bitcast(I32))
+        gather_words("b", list_b)
+
+        wa_code = [keep.tile([P, N], U32, name=f"wa_code{z}", align_bytes=64) for z in range(PASSES)]
+        wa_scale = [keep.tile([P, N], U8, name=f"wa_scale{z}", align_bytes=64) for z in range(PASSES)]
+        mh = P // HALVES
+        for z in range(PASSES):
+            grouped = keep.tile([P, N * PACK], BF16, name=f"wa_bf{z}", align_bytes=64)
+            dealt = grouped[:].rearrange("p (t m j) -> p m t j", t=PACK, j=PACK)
+            for h in range(HALVES):
+                src = wa_raw[z, h][:].rearrange("p j (m t) -> p m t j", t=PACK)
+                dst = dealt[:, h * mh : (h + 1) * mh, :, :]
+                if (z, h) == (PASSES - 1, HALVES - 1):
+                    nc.gpsimd.tensor_scalar(dst, src, 1.0, 0.0, ALU.mult, ALU.add)
+                else:
+                    nc.scalar.copy(dst, src)
+            nc.vector.quantize_mx(out=wa_code[z][:].bitcast(FP8X4), scales=wa_scale[z][:], in_=grouped[:])
+
+        res_s = [keep.tile([P, T], F32, name=f"res_s{t}") for t in range(PACK)]
+        for t in range(PACK):
+            res_raw = keep.tile([P, T], F32, name=f"stage{t}")
+            nc.sync.dma_start(res_raw[:], res_rows[:, t, :])
+            nc.gpsimd.tensor_scalar(res_s[t][:], res_raw[:], RES_WEIGHT, 0.0, ALU.mult, ALU.add)
+
+        p_slot = [keep.tile([P, J], F32, name=f"p_slot{t}") for t in range(PACK)]
+        q_slot = [keep.tile([P, J], F32, name=f"q_slot{t}") for t in range(PACK)]
+        q_turned = [keep.tile([P, N], F32, name=f"q_turned{s}") for s in range(PACK)]
+
+        def first_expert(t):
+            acc = psum.tile([P, J], F32, name="p_acc")
+            cols = slice(t * P, (t + 1) * P)
+            for z in range(PASSES):
+                nc.tensor.matmul_mx(
+                    out=acc[:],
+                    lhsT=wa_code[z][:, cols].bitcast(FP8X4),
+                    lhsT_scale=wa_scale[z][:, cols],
+                    rhs=g_word["a", z][:].bitcast(FP4X4),
+                    rhs_scale=g_scale[z][:, 0:J],
+                    start=(z == 0),
+                    stop=(z == PASSES - 1),
+                )
+            nc.scalar.copy(p_slot[t][:], acc[:])
+
+        def second_expert(s):
+            acc = psum_qt.tile([P, N], F32, name="qt_acc")
+            for z in range(PASSES):
+                nc.tensor.matmul_mx(
+                    out=acc[:],
+                    lhsT=g_word["b", z][:, 2 * s * P : 2 * (s + 1) * P].bitcast(FP4X4),
+                    lhsT_scale=g_scale[z][:, J + s * P : J + (s + 1) * P],
+                    rhs=wb_word[:, z, :].bitcast(FP8X4),
+                    rhs_scale=wb_scale[:, z, :],
+                    start=(z == 0),
+                    stop=(z == PASSES - 1),
+                )
+            nc.scalar.activation(
+                q_turned[s][:].rearrange("p (t m) -> p t m", t=PACK),
+                acc[:].rearrange("p (m t) -> p t m", t=PACK),
+                ACT.Copy,
+                scale=gate[:, s : s + 1],
+            )
+
+        def turn_back(t):
+            acc = psum.tile([P, J], F32, name="q_acc")
+            for s in range(PACK):
+                nc.tensor.transpose(acc[:, s * P : (s + 1) * P], q_turned[s][:, t * P : (t + 1) * P], ident[:])
+            nc.scalar.copy(q_slot[t][:], acc[:])
+
+        first_expert(0)
+        for s in range(PACK):
+            second_expert(s)
+        turn_back(0)
+        for t in range(1, PACK):
+            first_expert(t)
+            turn_back(t)
+
+        y = keep.tile([P, PACK, T], F32, name="y")
+        y_code = keep.tile([P, T], U32, name="y_code", align_bytes=64)
+        y_scale = keep.tile([P, T], U8, name="y_scale", align_bytes=64)
+        code_rows = out_1[0].rearrange("p c r -> p (c r)").bitcast(I32)
+        cw = T // CHUNKS
+        for t in range(PACK):
+            pg, qg = p_win[t % 2], q_win[t % 2]
+            nc.vector.tensor_copy(pg[:].indirect(list_a[:]), p_slot[t][:])
+            size = ring.tile([P, T], F32, name="size")
+            nc.scalar.activation(size[:], pg[:], ACT.Abs)
+            weak = ring.tile([P, T], F32, name="weak")
+            nc.scalar.activation(weak[:], size[:], ACT.Exp, scale=-1.0)
+            base = ring.tile([P, T], F32, name="base")
+            nc.gpsimd.tensor_tensor(base[:], pg[:], res_s[t][:], ALU.add)
+            nc.vector.tensor_copy(qg[:].indirect(list_b[:]), q_slot[t][:])
+            extra = ring.tile([P, T], F32, name="extra")
+            if t < PACK - 1:
+                nc.gpsimd.tensor_tensor(extra[:], qg[:], weak[:], ALU.mult)
+                nc.gpsimd.tensor_tensor(y[:, t, :], base[:], extra[:], ALU.add)
+                nc.sync.dma_start(out_rows[:, t, :], y[:, t, :])
+            else:
+                for c in range(CHUNKS):
+                    cols = slice(c * cw, (c + 1) * cw)
+                    nc.vector.tensor_tensor(extra[:, cols], qg[:, cols], weak[:, cols], ALU.mult)
+                    nc.vector.tensor_tensor(y[:, t, cols], base[:, cols], extra[:, cols], ALU.add)
+                    nc.sync.dma_start(out_rows[:, t, cols], y[:, t, cols])
+        for c in range(CHUNKS):
+            cols = slice(c * cw, (c + 1) * cw)
+            y_bf = keep.tile([P, cw * PACK], BF16, name=f"y_bf{c}", align_bytes=64)
+            nc.scalar.copy(
+                y_bf[:].rearrange("p (c i t) -> p c t i", i=4, t=PACK),
+                y[:, :, cols].rearrange("p t (c i) -> p c t i", i=4),
+            )
+            nc.vector.quantize_mx(out=y_code[:, cols].bitcast(FP8X4), scales=y_scale[:, cols], in_=y_bf[:])
+            nc.sync.dma_start(code_rows[:, cols], y_code[:, cols].bitcast(I32))
+        for q in range(QUADS):
+            eng = nc.sync if q % 2 == 0 else nc.scalar
+            eng.dma_start(out_2[0, 4 * q : 4 * q + 4, :].bitcast(I32), y_scale[32 * q : 32 * q + 4, :].bitcast(I32))

@@ -35,6 +35,7 @@ def tile_moe_second_choice_where_first_is_weak_pl_kernel(
         ring = ctx.enter_context(tc.tile_pool(name="ring", bufs=2))
         psum_qt = ctx.enter_context(tc.psum_pool(name="psum_qt", bufs=4))
         psum = ctx.enter_context(tc.psum_pool(name="psum", bufs=2))
+        psum_p = ctx.enter_context(tc.psum_pool(name="psum_p", bufs=1))
 
         list_a = keep.tile([P, J // 16], U16, name="list_a")
         list_b = keep.tile([P, J // 16], U16, name="list_b")
@@ -44,19 +45,17 @@ def tile_moe_second_choice_where_first_is_weak_pl_kernel(
         nc.sync.dma_start(list_a[:], offs)
         for z in range(PASSES):
             nc.sync.dma_start(x_word[z][:].bitcast(I32), xt_words[z].bitcast(I32))
-        nc.sync.dma_start(list_b[:], offs2)
         for q in range(QUADS):
             nc.scalar.dma_start(
                 x_scale[32 * q : 32 * q + 8, :].bitcast(I32), xt_scales[:, 4 * q : 4 * q + 4, :].bitcast(I32)
             )
 
         hw = N // HALVES
-        wa_raw = {}
-        for z in range(PASSES):
-            rows = wa[z * 512 : (z + 1) * 512, :].rearrange("(p j) c -> p j c", j=PACK)
-            for h in range(HALVES):
-                wa_raw[z, h] = keep.tile([P, PACK, hw], F32, name=f"stage{HALVES * z + h}")
-                nc.sync.dma_start(wa_raw[z, h][:], rows[:, :, h * hw : (h + 1) * hw])
+        wa_raw = [keep.tile([P, PACK, N], F32, name=f"stage{z}") for z in range(PASSES)]
+        wa_rows = wa.rearrange("(z p j) c -> z p j c", p=P, j=PACK)
+        nc.sync.dma_start(wa_raw[0][:], wa_rows[0])
+        nc.sync.dma_start(list_b[:], offs2)
+        nc.sync.dma_start(wa_raw[1][:], wa_rows[1])
 
         wb_word = keep.tile([P, PASSES, N], I32, name="wb_word", align_bytes=64)
         wb_scale = keep.tile([P, PASSES, N], U8, name="wb_scale", align_bytes=64)
@@ -75,7 +74,7 @@ def tile_moe_second_choice_where_first_is_weak_pl_kernel(
 
         p_win = [keep.tile([P, T], F32, name=f"p_win{i}") for i in range(2)]
         q_win = [keep.tile([P, T], F32, name=f"q_win{i}") for i in range(2)]
-        for w in (p_win[0], q_win[0], p_win[1], q_win[1]):
+        for w in (p_win[0], q_win[0]):
             nc.vector.memset(w[:], 0.0)
         ident = keep.tile([P, P], F32, name="ident")
         make_identity(nc, ident[:])
@@ -86,16 +85,15 @@ def tile_moe_second_choice_where_first_is_weak_pl_kernel(
         g_scale = [g_scale0, g_scale1]
         g_word = {}
 
-        def gather_words(name, lst):
-            for z in range(PASSES):
-                g_word[name, z] = keep.tile([P, 2 * J], U8, name=f"g_word_{name}{z}", align_bytes=64)
-                nc.vector.tensor_copy(g_word[name, z][:].bitcast(U16), x_word[z][:].bitcast(U16).indirect(lst[:]))
+        def gather_words(name, lst, z, tag):
+            g_word[name, z] = keep.tile([P, 2 * J], U8, name=f"g_word_{name}{z}", tag=tag, align_bytes=64)
+            nc.vector.tensor_copy(g_word[name, z][:].bitcast(U16), x_word[z][:].bitcast(U16).indirect(lst[:]))
 
-        gather_words("a", list_a)
         nc.vector.tensor_copy(g_scale0[:, 0:J], x_scale[:].indirect(list_a[:]))
         nc.vector.tensor_copy(g_scale0[:, J : 2 * J], x_scale[:].indirect(list_b[:]))
-        nc.gpsimd.dma_start(g_scale1[0:112, :].bitcast(I32), g_scale0[4:116, :].bitcast(I32))
-        gather_words("b", list_b)
+        nc.sync.dma_start(g_scale1[0:112, :].bitcast(I32), g_scale0[4:116, :].bitcast(I32))
+        for z in range(PASSES):
+            gather_words("a", list_a, z, f"g_word_a{z}")
 
         wa_code = [keep.tile([P, N], U32, name=f"wa_code{z}", align_bytes=64) for z in range(PASSES)]
         wa_scale = [keep.tile([P, N], U8, name=f"wa_scale{z}", align_bytes=64) for z in range(PASSES)]
@@ -104,106 +102,146 @@ def tile_moe_second_choice_where_first_is_weak_pl_kernel(
             grouped = keep.tile([P, N * PACK], BF16, name=f"wa_bf{z}", align_bytes=64)
             dealt = grouped[:].rearrange("p (t m j) -> p m t j", t=PACK, j=PACK)
             for h in range(HALVES):
-                src = wa_raw[z, h][:].rearrange("p j (m t) -> p m t j", t=PACK)
+                src = wa_raw[z][:, :, h * hw : (h + 1) * hw].rearrange("p j (m t) -> p m t j", t=PACK)
                 dst = dealt[:, h * mh : (h + 1) * mh, :, :]
-                if (z, h) == (PASSES - 1, HALVES - 1):
+                if h == 1:
                     nc.gpsimd.tensor_scalar(dst, src, 1.0, 0.0, ALU.mult, ALU.add)
                 else:
                     nc.scalar.copy(dst, src)
             nc.vector.quantize_mx(out=wa_code[z][:].bitcast(FP8X4), scales=wa_scale[z][:], in_=grouped[:])
+            gather_words("b", list_b, z, f"wa_bf{z}")
 
+        for w in (p_win[1], q_win[1]):
+            nc.gpsimd.memset(w[:], 0.0)
         res_s = [keep.tile([P, T], F32, name=f"res_s{t}") for t in range(PACK)]
-        for t in range(PACK):
-            res_raw = keep.tile([P, T], F32, name=f"stage{t}")
-            nc.sync.dma_start(res_raw[:], res_rows[:, t, :])
-            nc.gpsimd.tensor_scalar(res_s[t][:], res_raw[:], RES_WEIGHT, 0.0, ALU.mult, ALU.add)
+        for z in range(2):
+            res_raw = keep.tile([P, 2, T], F32, name=f"stage{z}")
+            nc.sync.dma_start(res_raw[:], res_rows[:, 2 * z : 2 * z + 2, :])
+            for t in range(2):
+                nc.gpsimd.tensor_scalar(res_s[2 * z + t][:], res_raw[:, t, :], RES_WEIGHT, 0.0, ALU.mult, ALU.add)
 
-        p_slot = [keep.tile([P, J], F32, name=f"p_slot{t}") for t in range(PACK)]
+        q_turned = keep.tile([P, PACK, PACK, P], F32, name="q_turned")
+        spare = q_turned[:].rearrange("p t s m -> p (t s m)")
+        p_slot = [keep.tile([P, J], F32, name=f"p_slot{t}")[:] if t != 1 else spare[:, 0:J] for t in range(PACK)]
         q_slot = [keep.tile([P, J], F32, name=f"q_slot{t}") for t in range(PACK)]
-        q_turned = [keep.tile([P, N], F32, name=f"q_turned{s}") for s in range(PACK)]
+
+        def first_pass(acc, t, z):
+            cols = slice(t * P, (t + 1) * P)
+            nc.tensor.matmul_mx(
+                out=acc[:],
+                lhsT=wa_code[z][:, cols].bitcast(FP8X4),
+                lhsT_scale=wa_scale[z][:, cols],
+                rhs=g_word["a", z][:].bitcast(FP4X4),
+                rhs_scale=g_scale[z][:, 0:J],
+                start=(z == 0),
+                stop=(z == PASSES - 1),
+            )
 
         def first_expert(t):
-            acc = psum.tile([P, J], F32, name="p_acc")
-            cols = slice(t * P, (t + 1) * P)
+            acc = psum_p.tile([P, J], F32, name="p_acc")
             for z in range(PASSES):
-                nc.tensor.matmul_mx(
-                    out=acc[:],
-                    lhsT=wa_code[z][:, cols].bitcast(FP8X4),
-                    lhsT_scale=wa_scale[z][:, cols],
-                    rhs=g_word["a", z][:].bitcast(FP4X4),
-                    rhs_scale=g_scale[z][:, 0:J],
-                    start=(z == 0),
-                    stop=(z == PASSES - 1),
-                )
-            nc.scalar.copy(p_slot[t][:], acc[:])
+                first_pass(acc, t, z)
+            nc.scalar.copy(p_slot[t], acc[:])
 
-        def second_expert(s):
-            acc = psum_qt.tile([P, N], F32, name="qt_acc")
-            for z in range(PASSES):
-                nc.tensor.matmul_mx(
-                    out=acc[:],
-                    lhsT=g_word["b", z][:, 2 * s * P : 2 * (s + 1) * P].bitcast(FP4X4),
-                    lhsT_scale=g_scale[z][:, J + s * P : J + (s + 1) * P],
-                    rhs=wb_word[:, z, :].bitcast(FP8X4),
-                    rhs_scale=wb_scale[:, z, :],
-                    start=(z == 0),
-                    stop=(z == PASSES - 1),
-                )
-            nc.scalar.activation(
-                q_turned[s][:].rearrange("p (t m) -> p t m", t=PACK),
-                acc[:].rearrange("p (m t) -> p t m", t=PACK),
-                ACT.Copy,
-                scale=gate[:, s : s + 1],
+        def second_pass(acc, s, z):
+            nc.tensor.matmul_mx(
+                out=acc[:],
+                lhsT=g_word["b", z][:, 2 * s * P : 2 * (s + 1) * P].bitcast(FP4X4),
+                lhsT_scale=g_scale[z][:, J + s * P : J + (s + 1) * P],
+                rhs=wb_word[:, z, :].bitcast(FP8X4),
+                rhs_scale=wb_scale[:, z, :],
+                start=(z == 0),
+                stop=(z == PASSES - 1),
             )
 
         def turn_back(t):
             acc = psum.tile([P, J], F32, name="q_acc")
             for s in range(PACK):
-                nc.tensor.transpose(acc[:, s * P : (s + 1) * P], q_turned[s][:, t * P : (t + 1) * P], ident[:])
-            nc.scalar.copy(q_slot[t][:], acc[:])
-
-        first_expert(0)
-        for s in range(PACK):
-            second_expert(s)
-        turn_back(0)
-        for t in range(1, PACK):
-            first_expert(t)
-            turn_back(t)
+                nc.tensor.transpose(acc[:, s * P : (s + 1) * P], q_turned[:, t, s, :], ident[:])
+            return acc
 
         y = keep.tile([P, PACK, T], F32, name="y")
         y_code = keep.tile([P, T], U32, name="y_code", align_bytes=64)
         y_scale = keep.tile([P, T], U8, name="y_scale", align_bytes=64)
         code_rows = out_1[0].rearrange("p c r -> p (c r)").bitcast(I32)
         cw = T // CHUNKS
-        for t in range(PACK):
-            pg, qg = p_win[t % 2], q_win[t % 2]
-            nc.vector.tensor_copy(pg[:].indirect(list_a[:]), p_slot[t][:])
-            size = ring.tile([P, T], F32, name="size")
-            nc.scalar.activation(size[:], pg[:], ACT.Abs)
-            weak = ring.tile([P, T], F32, name="weak")
-            nc.scalar.activation(weak[:], size[:], ACT.Exp, scale=-1.0)
-            base = ring.tile([P, T], F32, name="base")
-            nc.gpsimd.tensor_tensor(base[:], pg[:], res_s[t][:], ALU.add)
+        weak, base = {}, {}
+
+        def place_first(t):
+            pg = p_win[t % 2]
+            nc.vector.tensor_copy(pg[:].indirect(list_a[:]), p_slot[t])
+            if t == 0:
+                size = spare[:, J : J + T]
+            elif t == PACK - 1:
+                size = y[:, 0, :]
+            else:
+                size = keep.tile([P, T], F32, name="size")[:]
+            nc.scalar.activation(size, pg[:], ACT.Abs)
+            weak[t] = ring.tile([P, T], F32, name="weak")
+            nc.scalar.activation(weak[t][:], size, ACT.Exp, scale=-1.0)
+            base[t] = keep.tile([P, T], F32, name="base")
+            nc.gpsimd.tensor_tensor(base[t][:], pg[:], res_s[t][:], ALU.add)
+
+        def place_second(t):
+            qg = q_win[t % 2]
             nc.vector.tensor_copy(qg[:].indirect(list_b[:]), q_slot[t][:])
-            extra = ring.tile([P, T], F32, name="extra")
+            extra = keep.tile([P, T], F32, name="extra")
             if t < PACK - 1:
-                nc.gpsimd.tensor_tensor(extra[:], qg[:], weak[:], ALU.mult)
-                nc.gpsimd.tensor_tensor(y[:, t, :], base[:], extra[:], ALU.add)
+                nc.gpsimd.tensor_tensor(extra[:], qg[:], weak[t][:], ALU.mult)
+                nc.gpsimd.tensor_tensor(y[:, t, :], base[t][:], extra[:], ALU.add)
                 nc.sync.dma_start(out_rows[:, t, :], y[:, t, :])
             else:
                 for c in range(CHUNKS):
                     cols = slice(c * cw, (c + 1) * cw)
-                    nc.vector.tensor_tensor(extra[:, cols], qg[:, cols], weak[:, cols], ALU.mult)
-                    nc.vector.tensor_tensor(y[:, t, cols], base[:, cols], extra[:, cols], ALU.add)
+                    nc.vector.tensor_tensor(extra[:, cols], qg[:, cols], weak[t][:, cols], ALU.mult)
+                    nc.vector.tensor_tensor(y[:, t, cols], base[t][:, cols], extra[:, cols], ALU.add)
                     nc.sync.dma_start(out_rows[:, t, cols], y[:, t, cols])
+
+        p_acc = psum_p.tile([P, J], F32, name="p_acc")
+        qt_acc = [psum_qt.tile([P, N], F32, name="qt_acc") for s in range(PACK)]
+        for z in range(PASSES):
+            first_pass(p_acc, 0, z)
+            for s in range(PACK):
+                second_pass(qt_acc[s], s, z)
+        nc.scalar.copy(p_slot[0], p_acc[:])
+        for s in range(PACK):
+            nc.scalar.activation(
+                q_turned[:, :, s, :],
+                qt_acc[s][:].rearrange("p (m t) -> p t m", t=PACK),
+                ACT.Copy,
+                scale=gate[:, s : s + 1],
+            )
+        q_acc = {0: turn_back(0)}
+        nc.scalar.copy(q_slot[0][:], q_acc[0][:])
+        first_expert(1)
+        q_acc[1] = turn_back(1)
+        q_acc[2] = turn_back(2)
+        place_first(0)
+        nc.scalar.copy(q_slot[1][:], q_acc[1][:])
+        first_expert(2)
+        nc.scalar.copy(q_slot[2][:], q_acc[2][:])
+        q_acc[3] = turn_back(3)
+        first_expert(3)
+        nc.scalar.copy(q_slot[3][:], q_acc[3][:])
+        place_second(0)
+        y_bf = [keep.tile([P, cw, PACK], BF16, name=f"y_bf{c}", align_bytes=64) for c in range(CHUNKS)]
+
+        def round_pair(c, t0):
+            cols = slice(c * cw, (c + 1) * cw)
+            nc.scalar.copy(y_bf[c][:, :, t0 : t0 + 2], y[:, t0 : t0 + 2, cols].rearrange("p t c -> p c t"))
+
+        for t in range(1, PACK):
+            place_first(t)
+            if t == 2:
+                for c in range(CHUNKS):
+                    round_pair(c, 0)
+            place_second(t)
         for c in range(CHUNKS):
             cols = slice(c * cw, (c + 1) * cw)
-            y_bf = keep.tile([P, cw * PACK], BF16, name=f"y_bf{c}", align_bytes=64)
-            nc.scalar.copy(
-                y_bf[:].rearrange("p (c i t) -> p c t i", i=4, t=PACK),
-                y[:, :, cols].rearrange("p t (c i) -> p c t i", i=4),
+            round_pair(c, 2)
+            nc.vector.quantize_mx(
+                out=y_code[:, cols].bitcast(FP8X4), scales=y_scale[:, cols], in_=y_bf[c][:].rearrange("p c t -> p (c t)")
             )
-            nc.vector.quantize_mx(out=y_code[:, cols].bitcast(FP8X4), scales=y_scale[:, cols], in_=y_bf[:])
             nc.sync.dma_start(code_rows[:, cols], y_code[:, cols].bitcast(I32))
         for q in range(QUADS):
             eng = nc.sync if q % 2 == 0 else nc.scalar

@@ -72,9 +72,9 @@ def tile_moe_second_choice_where_first_is_weak_pl_kernel(
         res_rows = res.rearrange("(p t) c -> p t c", t=PACK)
         out_rows = out_0.rearrange("(p t) c -> p t c", t=PACK)
 
-        p_win = [keep.tile([P, T], F32, name=f"p_win{i}") for i in range(2)]
+        p_win = [keep.tile([P, T], F32, name=f"p_win{i}") for i in range(3)]
         q_win = [keep.tile([P, T], F32, name=f"q_win{i}") for i in range(2)]
-        for w in (p_win[0], q_win[0]):
+        for w in (p_win[0], q_win[0], p_win[1]):
             nc.vector.memset(w[:], 0.0)
         ident = keep.tile([P, P], F32, name="ident")
         make_identity(nc, ident[:])
@@ -111,14 +111,16 @@ def tile_moe_second_choice_where_first_is_weak_pl_kernel(
             nc.vector.quantize_mx(out=wa_code[z][:].bitcast(FP8X4), scales=wa_scale[z][:], in_=grouped[:])
             gather_words("b", list_b, z, f"wa_bf{z}")
 
-        for w in (p_win[1], q_win[1]):
+        for w in (q_win[1], p_win[2]):
             nc.gpsimd.memset(w[:], 0.0)
-        res_s = [keep.tile([P, T], F32, name=f"res_s{t}") for t in range(PACK)]
+        res_s = [keep.tile([P, T], F32, name=f"res_s{t}") for t in range(PACK - 1)]
         for z in range(2):
             res_raw = keep.tile([P, 2, T], F32, name=f"stage{z}")
             nc.sync.dma_start(res_raw[:], res_rows[:, 2 * z : 2 * z + 2, :])
             for t in range(2):
-                nc.gpsimd.tensor_scalar(res_s[2 * z + t][:], res_raw[:, t, :], RES_WEIGHT, 0.0, ALU.mult, ALU.add)
+                if 2 * z + t < PACK - 1:
+                    nc.gpsimd.tensor_scalar(res_s[2 * z + t][:], res_raw[:, t, :], RES_WEIGHT, 0.0, ALU.mult, ALU.add)
+        res_last = res_raw[:, 1, :]
 
         q_turned = keep.tile([P, PACK, PACK, P], F32, name="q_turned")
         spare = q_turned[:].rearrange("p t s m -> p (t s m)")
@@ -164,39 +166,75 @@ def tile_moe_second_choice_where_first_is_weak_pl_kernel(
         y_code = keep.tile([P, T], U32, name="y_code", align_bytes=64)
         y_scale = keep.tile([P, T], U8, name="y_scale", align_bytes=64)
         code_rows = out_1[0].rearrange("p c r -> p (c r)").bitcast(I32)
-        cw = T // CHUNKS
+        edges = [0, 512, 768, 896, 1024]
+        chunks = [slice(a, b) for a, b in zip(edges, edges[1:])]
         weak, base = {}, {}
+        turned = keep.tile([P, T], F32, name="turned")
+        bank = T // 2
+
+        def sum_on_tensor(terms, staging):
+            for h in range(2):
+                fwd = psum_qt.tile([P, bank], F32, name="qt_acc")
+                for b in range(PACK):
+                    cols = slice(h * bank + b * P, h * bank + (b + 1) * P)
+                    for i, term in enumerate(terms):
+                        nc.tensor.matmul(
+                            fwd[:, b * P : (b + 1) * P], term[:, cols], ident[:],
+                            is_transpose=True, start=(i == 0), stop=(i == len(terms) - 1),
+                        )
+                nc.scalar.copy(staging[:, h * bank : (h + 1) * bank], fwd[:])
+            back = []
+            for h in range(2):
+                bk = psum_qt.tile([P, bank], F32, name="qt_acc")
+                for b in range(PACK):
+                    cols = slice(h * bank + b * P, h * bank + (b + 1) * P)
+                    nc.tensor.transpose(bk[:, b * P : (b + 1) * P], staging[:, cols], ident[:])
+                back.append(bk)
+            return back
 
         def place_first(t):
-            pg = p_win[t % 2]
+            pg = p_win[t % 3]
             nc.vector.tensor_copy(pg[:].indirect(list_a[:]), p_slot[t])
-            if t == 0:
-                size = spare[:, J : J + T]
-            elif t == PACK - 1:
-                size = y[:, 0, :]
-            else:
-                size = keep.tile([P, T], F32, name="size")[:]
+            size = [spare[:, J : J + T], size_one[:], turned[:], y[:, 0, :]][t]
             nc.scalar.activation(size, pg[:], ACT.Abs)
             weak[t] = ring.tile([P, T], F32, name="weak")
             nc.scalar.activation(weak[t][:], size, ACT.Exp, scale=-1.0)
-            base[t] = keep.tile([P, T], F32, name="base")
-            nc.gpsimd.tensor_tensor(base[t][:], pg[:], res_s[t][:], ALU.add)
+            if t in (1, 2):
+                base[t] = ring.tile([P, T], F32, name="weak")
+                nc.gpsimd.tensor_tensor(base[t][:], pg[:], res_s[t][:], ALU.add)
 
         def place_second(t):
             qg = q_win[t % 2]
             nc.vector.tensor_copy(qg[:].indirect(list_b[:]), q_slot[t][:])
-            extra = keep.tile([P, T], F32, name="extra")
-            if t < PACK - 1:
+            extra = keep.tile([P, T], F32, name="extra_first" if t == 0 else "extra")
+            if t == 0:
+                nc.gpsimd.tensor_tensor(extra[:], qg[:], weak[t][:], ALU.mult)
+                back = sum_on_tensor([p_win[0][:], res_s[0][:], extra[:]], turned[:])
+                for h in range(2):
+                    nc.scalar.copy(y[:, t, h * bank : (h + 1) * bank], back[h][:])
+                nc.sync.dma_start(out_rows[:, t, :], y[:, t, :])
+            elif t < PACK - 1:
                 nc.gpsimd.tensor_tensor(extra[:], qg[:], weak[t][:], ALU.mult)
                 nc.gpsimd.tensor_tensor(y[:, t, :], base[t][:], extra[:], ALU.add)
                 nc.sync.dma_start(out_rows[:, t, :], y[:, t, :])
             else:
-                for c in range(CHUNKS):
-                    cols = slice(c * cw, (c + 1) * cw)
+                last_base = keep.tile([P, T], F32, name="last_base")
+                for c, cols in enumerate(chunks):
                     nc.vector.tensor_tensor(extra[:, cols], qg[:, cols], weak[t][:, cols], ALU.mult)
-                    nc.vector.tensor_tensor(y[:, t, cols], base[t][:, cols], extra[:, cols], ALU.add)
+                    nc.vector.scalar_tensor_tensor(
+                        last_base[:, cols], res_last[:, cols], RES_WEIGHT, extra[:, cols], ALU.mult, ALU.add
+                    )
+                    nc.vector.tensor_tensor(y[:, t, cols], last_base[:, cols], p_win[t % 3][:, cols], ALU.add)
                     nc.sync.dma_start(out_rows[:, t, cols], y[:, t, cols])
+                    round_pair(c, 2)
+                    nc.vector.quantize_mx(
+                        out=y_code[:, cols].bitcast(FP8X4),
+                        scales=y_scale[:, cols],
+                        in_=y_bf[c][:].rearrange("p c t -> p (c t)"),
+                    )
+                    nc.sync.dma_start(code_rows[:, cols], y_code[:, cols].bitcast(I32))
 
+        size_one = keep.tile([P, T], F32, name="size_one")
         p_acc = psum_p.tile([P, J], F32, name="p_acc")
         qt_acc = [psum_qt.tile([P, N], F32, name="qt_acc") for s in range(PACK)]
         for z in range(PASSES):
@@ -204,15 +242,20 @@ def tile_moe_second_choice_where_first_is_weak_pl_kernel(
             for s in range(PACK):
                 second_pass(qt_acc[s], s, z)
         nc.scalar.copy(p_slot[0], p_acc[:])
-        for s in range(PACK):
-            nc.scalar.activation(
-                q_turned[:, :, s, :],
-                qt_acc[s][:].rearrange("p (m t) -> p t m", t=PACK),
-                ACT.Copy,
-                scale=gate[:, s : s + 1],
-            )
+
+        def gate_and_deal(ts):
+            for s in range(PACK):
+                nc.scalar.activation(
+                    q_turned[:, ts, s, :],
+                    qt_acc[s][:].rearrange("p (m t) -> p t m", t=PACK)[:, ts, :],
+                    ACT.Copy,
+                    scale=gate[:, s : s + 1],
+                )
+
+        gate_and_deal(slice(0, 1))
         q_acc = {0: turn_back(0)}
         nc.scalar.copy(q_slot[0][:], q_acc[0][:])
+        gate_and_deal(slice(1, PACK))
         first_expert(1)
         q_acc[1] = turn_back(1)
         q_acc[2] = turn_back(2)
@@ -224,10 +267,10 @@ def tile_moe_second_choice_where_first_is_weak_pl_kernel(
         first_expert(3)
         nc.scalar.copy(q_slot[3][:], q_acc[3][:])
         place_second(0)
-        y_bf = [keep.tile([P, cw, PACK], BF16, name=f"y_bf{c}", align_bytes=64) for c in range(CHUNKS)]
+        y_bf = [keep.tile([P, s.stop - s.start, PACK], BF16, name=f"y_bf{c}", align_bytes=64) for c, s in enumerate(chunks)]
 
         def round_pair(c, t0):
-            cols = slice(c * cw, (c + 1) * cw)
+            cols = chunks[c]
             nc.scalar.copy(y_bf[c][:, :, t0 : t0 + 2], y[:, t0 : t0 + 2, cols].rearrange("p t c -> p c t"))
 
         for t in range(1, PACK):
@@ -236,13 +279,6 @@ def tile_moe_second_choice_where_first_is_weak_pl_kernel(
                 for c in range(CHUNKS):
                     round_pair(c, 0)
             place_second(t)
-        for c in range(CHUNKS):
-            cols = slice(c * cw, (c + 1) * cw)
-            round_pair(c, 2)
-            nc.vector.quantize_mx(
-                out=y_code[:, cols].bitcast(FP8X4), scales=y_scale[:, cols], in_=y_bf[c][:].rearrange("p c t -> p (c t)")
-            )
-            nc.sync.dma_start(code_rows[:, cols], y_code[:, cols].bitcast(I32))
         for q in range(QUADS):
             eng = nc.sync if q % 2 == 0 else nc.scalar
             eng.dma_start(out_2[0, 4 * q : 4 * q + 4, :].bitcast(I32), y_scale[32 * q : 32 * q + 4, :].bitcast(I32))

@@ -41,21 +41,26 @@ def tile_moe_second_choice_where_first_is_weak_pl_kernel(
         list_b = keep.tile([P, J // 16], U16, name="list_b")
         x_scale = keep.tile([P, T], U8, name="x_scale", align_bytes=64)
         x_word = [keep.tile([P, 2 * T], U8, name=f"x_word{z}", align_bytes=64) for z in range(PASSES)]
-        nc.vector.memset(x_scale[:].bitcast(I32), 0)
+        nc.gpsimd.memset(x_scale[:].bitcast(I32), 0)
+        warm = keep.tile([P, 2], F32, name="warm")
+        nc.gpsimd.memset(warm[:, 0:1], 0.0)
+        nc.scalar.activation(warm[:, 1:2], warm[:, 0:1], ACT.Exp)
         nc.sync.dma_start(list_a[:], offs)
         for z in range(PASSES):
             nc.sync.dma_start(x_word[z][:].bitcast(I32), xt_words[z].bitcast(I32))
         for q in range(QUADS):
-            nc.scalar.dma_start(
+            nc.sync.dma_start(
                 x_scale[32 * q : 32 * q + 8, :].bitcast(I32), xt_scales[:, 4 * q : 4 * q + 4, :].bitcast(I32)
             )
 
         hw = N // HALVES
-        wa_raw = [keep.tile([P, PACK, N], F32, name=f"stage{z}") for z in range(PASSES)]
+        wa_first = keep.tile([P, PACK, N], F32, name="stage0")
+        wa_second = [keep.tile([P, PACK, hw], F32, name=f"stage{1 + h}") for h in range(HALVES)]
         wa_rows = wa.rearrange("(z p j) c -> z p j c", p=P, j=PACK)
-        nc.sync.dma_start(wa_raw[0][:], wa_rows[0])
+        nc.sync.dma_start(wa_first[:], wa_rows[0])
         nc.sync.dma_start(list_b[:], offs2)
-        nc.sync.dma_start(wa_raw[1][:], wa_rows[1])
+        for h in range(HALVES):
+            nc.sync.dma_start(wa_second[h][:], wa_rows[1][:, :, h * hw : (h + 1) * hw])
 
         wb_word = keep.tile([P, PASSES, N], I32, name="wb_word", align_bytes=64)
         wb_scale = keep.tile([P, PASSES, N], U8, name="wb_scale", align_bytes=64)
@@ -72,8 +77,8 @@ def tile_moe_second_choice_where_first_is_weak_pl_kernel(
         res_rows = res.rearrange("(p t) c -> p t c", t=PACK)
         out_rows = out_0.rearrange("(p t) c -> p t c", t=PACK)
 
-        p_win = [keep.tile([P, T], F32, name=f"p_win{i}") for i in range(3)]
-        q_win = [keep.tile([P, T], F32, name=f"q_win{i}") for i in range(2)]
+        p_win = [keep.tile([P, T], F32, name=f"p_win{i}") for i in range(2)]
+        q_win = [keep.tile([P, T], F32, name="q_win0")]
         for w in (p_win[0], q_win[0], p_win[1]):
             nc.vector.memset(w[:], 0.0)
         ident = keep.tile([P, P], F32, name="ident")
@@ -85,15 +90,16 @@ def tile_moe_second_choice_where_first_is_weak_pl_kernel(
         g_scale = [g_scale0, g_scale1]
         g_word = {}
 
-        def gather_words(name, lst, z, tag):
-            g_word[name, z] = keep.tile([P, 2 * J], U8, name=f"g_word_{name}{z}", tag=tag, align_bytes=64)
-            nc.vector.tensor_copy(g_word[name, z][:].bitcast(U16), x_word[z][:].bitcast(U16).indirect(lst[:]))
+        def gather_words(name, z, words, lst):
+            g_word[name, z] = words
+            nc.vector.tensor_copy(words.bitcast(U16), x_word[z][:].bitcast(U16).indirect(lst[:]))
 
+        words_a = keep.tile([P, PASSES, 2 * J], U8, name="words_a", align_bytes=64)
         nc.vector.tensor_copy(g_scale0[:, 0:J], x_scale[:].indirect(list_a[:]))
         nc.vector.tensor_copy(g_scale0[:, J : 2 * J], x_scale[:].indirect(list_b[:]))
         nc.sync.dma_start(g_scale1[0:112, :].bitcast(I32), g_scale0[4:116, :].bitcast(I32))
         for z in range(PASSES):
-            gather_words("a", list_a, z, f"g_word_a{z}")
+            gather_words("a", z, words_a[:, z, :], list_a)
 
         wa_code = [keep.tile([P, N], U32, name=f"wa_code{z}", align_bytes=64) for z in range(PASSES)]
         wa_scale = [keep.tile([P, N], U8, name=f"wa_scale{z}", align_bytes=64) for z in range(PASSES)]
@@ -102,25 +108,29 @@ def tile_moe_second_choice_where_first_is_weak_pl_kernel(
             grouped = keep.tile([P, N * PACK], BF16, name=f"wa_bf{z}", align_bytes=64)
             dealt = grouped[:].rearrange("p (t m j) -> p m t j", t=PACK, j=PACK)
             for h in range(HALVES):
-                src = wa_raw[z][:, :, h * hw : (h + 1) * hw].rearrange("p j (m t) -> p m t j", t=PACK)
+                raw = wa_first[:, :, h * hw : (h + 1) * hw] if z == 0 else wa_second[h][:]
+                src = raw.rearrange("p j (m t) -> p m t j", t=PACK)
                 dst = dealt[:, h * mh : (h + 1) * mh, :, :]
-                if h == 1:
+                if h == 0:
+                    nc.scalar.copy(dst, src)
+                elif z == 0:
                     nc.gpsimd.tensor_scalar(dst, src, 1.0, 0.0, ALU.mult, ALU.add)
                 else:
-                    nc.scalar.copy(dst, src)
+                    nc.vector.tensor_copy(dst, src)
             nc.vector.quantize_mx(out=wa_code[z][:].bitcast(FP8X4), scales=wa_scale[z][:], in_=grouped[:])
-            gather_words("b", list_b, z, f"wa_bf{z}")
+            words_b = keep.tile([P, 2 * J], U8, name=f"words_b{z}", tag=f"wa_bf{z}", align_bytes=64)
+            gather_words("b", z, words_b[:], list_b)
 
-        for w in (q_win[1], p_win[2]):
-            nc.gpsimd.memset(w[:], 0.0)
+        q_win.append(keep.tile([P, T], F32, name="q_win1", tag="x_word1", align_bytes=64))
         res_s = [keep.tile([P, T], F32, name=f"res_s{t}") for t in range(PACK - 1)]
         for z in range(2):
-            res_raw = keep.tile([P, 2, T], F32, name=f"stage{z}")
+            res_raw = keep.tile([P, 2, T], F32, name=f"stage{z + 1}")
             nc.sync.dma_start(res_raw[:], res_rows[:, 2 * z : 2 * z + 2, :])
             for t in range(2):
                 if 2 * z + t < PACK - 1:
                     nc.gpsimd.tensor_scalar(res_s[2 * z + t][:], res_raw[:, t, :], RES_WEIGHT, 0.0, ALU.mult, ALU.add)
         res_last = res_raw[:, 1, :]
+        nc.gpsimd.memset(q_win[1][:], 0.0)
 
         q_turned = keep.tile([P, PACK, PACK, P], F32, name="q_turned")
         spare = q_turned[:].rearrange("p t s m -> p (t s m)")
@@ -133,7 +143,7 @@ def tile_moe_second_choice_where_first_is_weak_pl_kernel(
                 out=acc[:],
                 lhsT=wa_code[z][:, cols].bitcast(FP8X4),
                 lhsT_scale=wa_scale[z][:, cols],
-                rhs=g_word["a", z][:].bitcast(FP4X4),
+                rhs=g_word["a", z].bitcast(FP4X4),
                 rhs_scale=g_scale[z][:, 0:J],
                 start=(z == 0),
                 stop=(z == PASSES - 1),
@@ -166,7 +176,7 @@ def tile_moe_second_choice_where_first_is_weak_pl_kernel(
         y_code = keep.tile([P, T], U32, name="y_code", align_bytes=64)
         y_scale = keep.tile([P, T], U8, name="y_scale", align_bytes=64)
         code_rows = out_1[0].rearrange("p c r -> p (c r)").bitcast(I32)
-        edges = [0, 512, 768, 896, 1024]
+        edges = [0, 256, 512, 768, 1024]
         chunks = [slice(a, b) for a, b in zip(edges, edges[1:])]
         weak, base = {}, {}
         turned = keep.tile([P, T], F32, name="turned")
@@ -218,21 +228,34 @@ def tile_moe_second_choice_where_first_is_weak_pl_kernel(
                 nc.gpsimd.tensor_tensor(y[:, t, :], base[t][:], extra[:], ALU.add)
                 nc.sync.dma_start(out_rows[:, t, :], y[:, t, :])
             else:
-                last_base = keep.tile([P, T], F32, name="last_base")
+                last_base = keep.tile([P, T], F32, name="last_base", tag=f"q_slot{t}")
+
+                def product(c):
+                    nc.vector.tensor_tensor(extra[:, chunks[c]], qg[:, chunks[c]], weak[t][:, chunks[c]], ALU.mult)
+
+                product(0)
                 for c, cols in enumerate(chunks):
-                    nc.vector.tensor_tensor(extra[:, cols], qg[:, cols], weak[t][:, cols], ALU.mult)
                     nc.vector.scalar_tensor_tensor(
-                        last_base[:, cols], res_last[:, cols], RES_WEIGHT, extra[:, cols], ALU.mult, ALU.add
+                        last_base[:, cols], res_last[:, cols], RES_WEIGHT, p_win[t % 3][:, cols], ALU.mult, ALU.add
                     )
-                    nc.vector.tensor_tensor(y[:, t, cols], last_base[:, cols], p_win[t % 3][:, cols], ALU.add)
+                    if c + 1 < CHUNKS:
+                        product(c + 1)
+                    else:
+                        quantize_out(0)
+                    nc.vector.tensor_tensor(y[:, t, cols], last_base[:, cols], extra[:, cols], ALU.add)
                     nc.sync.dma_start(out_rows[:, t, cols], y[:, t, cols])
                     round_pair(c, 2)
-                    nc.vector.quantize_mx(
-                        out=y_code[:, cols].bitcast(FP8X4),
-                        scales=y_scale[:, cols],
-                        in_=y_bf[c][:].rearrange("p c t -> p (c t)"),
-                    )
-                    nc.sync.dma_start(code_rows[:, cols], y_code[:, cols].bitcast(I32))
+                for c in range(1, CHUNKS):
+                    quantize_out(c)
+
+        def quantize_out(c):
+            cols = chunks[c]
+            nc.vector.quantize_mx(
+                out=y_code[:, cols].bitcast(FP8X4),
+                scales=y_scale[:, cols],
+                in_=y_bf[c][:].rearrange("p c t -> p (c t)"),
+            )
+            nc.sync.dma_start(code_rows[:, cols], y_code[:, cols].bitcast(I32))
 
         size_one = keep.tile([P, T], F32, name="size_one")
         p_acc = psum_p.tile([P, J], F32, name="p_acc")
@@ -260,6 +283,8 @@ def tile_moe_second_choice_where_first_is_weak_pl_kernel(
         q_acc[1] = turn_back(1)
         q_acc[2] = turn_back(2)
         place_first(0)
+        p_win.append(keep.tile([P, T], F32, name="p_win2", tag="p_slot0"))
+        nc.gpsimd.memset(p_win[2][:], 0.0)
         nc.scalar.copy(q_slot[1][:], q_acc[1][:])
         first_expert(2)
         nc.scalar.copy(q_slot[2][:], q_acc[2][:])

from contextlib import ExitStack

import concourse.mybir as mybir
from concourse.masks import make_identity

K, T, J, N = 1024, 1024, 512, 512
FLOPS = 2 * 2 * K * N * J

F32 = mybir.dt.float32
BF16 = mybir.dt.bfloat16
I32 = mybir.dt.int32
U32 = mybir.dt.uint32
U16 = mybir.dt.uint16
U8 = mybir.dt.uint8
FP8X4 = mybir.dt.float8_e4m3fn_x4
FP4X4 = mybir.dt.float4_e2m1fn_x4
ALU = mybir.AluOpType
ACT = mybir.ActivationFunctionType

P = 128
PACK = 4
PASSES = K // (P * PACK)
QUADS = 4
HALVES = 2
CHUNKS = 4
RES_WEIGHT = 0.3


def tile_moe_second_choice_where_first_is_weak_pl_kernel(
    tc, xt_words, xt_scales, wa, wb_words, wb_scales, gb, res, offs, offs2, out_0, out_1, out_2
):
    nc = tc.nc
    with ExitStack() as ctx:
        keep = ctx.enter_context(tc.tile_pool(name="keep", bufs=1))
        ring = ctx.enter_context(tc.tile_pool(name="ring", bufs=2))
        psum_qt = ctx.enter_context(tc.psum_pool(name="psum_qt", bufs=4))
        psum = ctx.enter_context(tc.psum_pool(name="psum", bufs=2))
        psum_p = ctx.enter_context(tc.psum_pool(name="psum_p", bufs=1))

        list_a = keep.tile([P, J // 16], U16, name="list_a")
        list_b = keep.tile([P, J // 16], U16, name="list_b")
        x_scale = keep.tile([P, T], U8, name="x_scale", align_bytes=64)
        x_word = [keep.tile([P, 2 * T], U8, name=f"x_word{z}", align_bytes=64) for z in range(PASSES)]
        nc.gpsimd.memset(x_scale[:].bitcast(I32), 0)
        warm = keep.tile([P, 2], F32, name="warm")
        nc.gpsimd.memset(warm[:, 0:1], 0.0)
        nc.scalar.activation(warm[:, 1:2], warm[:, 0:1], ACT.Exp)
        nc.sync.dma_start(list_a[:], offs)
        for z in range(PASSES):
            nc.sync.dma_start(x_word[z][:].bitcast(I32), xt_words[z].bitcast(I32))
        for q in range(QUADS):
            nc.sync.dma_start(
                x_scale[32 * q : 32 * q + 8, :].bitcast(I32), xt_scales[:, 4 * q : 4 * q + 4, :].bitcast(I32)
            )

        hw = N // HALVES
        wa_first = keep.tile([P, PACK, N], F32, name="stage0")
        wa_second = [keep.tile([P, PACK, hw], F32, name=f"stage{1 + h}") for h in range(HALVES)]
        wa_rows = wa.rearrange("(z p j) c -> z p j c", p=P, j=PACK)
        nc.sync.dma_start(wa_first[:], wa_rows[0])
        nc.sync.dma_start(list_b[:], offs2)
        for h in range(HALVES):
            nc.sync.dma_start(wa_second[h][:], wa_rows[1][:, :, h * hw : (h + 1) * hw])

        wb_word = keep.tile([P, PASSES, N], I32, name="wb_word", align_bytes=64)
        wb_scale = keep.tile([P, PASSES, N], U8, name="wb_scale", align_bytes=64)
        nc.gpsimd.memset(wb_scale[:].bitcast(I32), 0)
        for q in range(QUADS):
            nc.sync.dma_start(
                wb_scale[32 * q : 32 * q + 4, :, :].bitcast(I32),
                wb_scales[:, 4 * q : 4 * q + 4, :].rearrange("z r n -> r z n").bitcast(I32),
            )
        nc.sync.dma_start(wb_word[:], wb_words.rearrange("z p n t -> p z (n t)").bitcast(I32))
        gate = keep.tile([P, PACK], F32, name="gate")
        with nc.allow_non_contiguous_dma(reason="one gate value a partition"):
            nc.sync.dma_start(gate[:], gb[0].rearrange("(s p) -> p s", p=P))
        res_rows = res.rearrange("(p t) c -> p t c", t=PACK)
        out_rows = out_0.rearrange("(p t) c -> p t c", t=PACK)

        p_win = [keep.tile([P, T], F32, name=f"p_win{i}") for i in range(2)]
        q_win = [keep.tile([P, T], F32, name="q_win0")]
        for w in (p_win[0], q_win[0], p_win[1]):
            nc.vector.memset(w[:], 0.0)
        ident = keep.tile([P, P], F32, name="ident")
        make_identity(nc, ident[:])

        g_scale0 = keep.tile([P, 2 * J], U8, name="g_scale0", align_bytes=64)
        g_scale1 = keep.tile([P, 2 * J], U8, name="g_scale1", align_bytes=64)
        nc.gpsimd.memset(g_scale1[:].bitcast(I32), 0)
        g_scale = [g_scale0, g_scale1]
        g_word = {}

        def gather_words(name, z, words, lst):
            g_word[name, z] = words
            nc.vector.tensor_copy(words.bitcast(U16), x_word[z][:].bitcast(U16).indirect(lst[:]))

        words_a = keep.tile([P, PASSES, 2 * J], U8, name="words_a", align_bytes=64)
        nc.vector.tensor_copy(g_scale0[:, 0:J], x_scale[:].indirect(list_a[:]))
        nc.vector.tensor_copy(g_scale0[:, J : 2 * J], x_scale[:].indirect(list_b[:]))
        nc.sync.dma_start(g_scale1[0:112, :].bitcast(I32), g_scale0[4:116, :].bitcast(I32))
        for z in range(PASSES):
            gather_words("a", z, words_a[:, z, :], list_a)

        wa_code = [keep.tile([P, N], U32, name=f"wa_code{z}", align_bytes=64) for z in range(PASSES)]
        wa_scale = [keep.tile([P, N], U8, name=f"wa_scale{z}", align_bytes=64) for z in range(PASSES)]
        mh = P // HALVES
        for z in range(PASSES):
            grouped = keep.tile([P, N * PACK], BF16, name=f"wa_bf{z}", align_bytes=64)
            dealt = grouped[:].rearrange("p (t m j) -> p m t j", t=PACK, j=PACK)
            for h in range(HALVES):
                raw = wa_first[:, :, h * hw : (h + 1) * hw] if z == 0 else wa_second[h][:]
                src = raw.rearrange("p j (m t) -> p m t j", t=PACK)
                dst = dealt[:, h * mh : (h + 1) * mh, :, :]
                if h == 0:
                    nc.scalar.copy(dst, src)
                elif z == 0:
                    nc.gpsimd.tensor_scalar(dst, src, 1.0, 0.0, ALU.mult, ALU.add)
                else:
                    nc.vector.tensor_copy(dst, src)
            nc.vector.quantize_mx(out=wa_code[z][:].bitcast(FP8X4), scales=wa_scale[z][:], in_=grouped[:])
            words_b = keep.tile([P, 2 * J], U8, name=f"words_b{z}", tag=f"wa_bf{z}", align_bytes=64)
            gather_words("b", z, words_b[:], list_b)

        q_win.append(keep.tile([P, T], F32, name="q_win1", tag="x_word1", align_bytes=64))
        res_s = [keep.tile([P, T], F32, name=f"res_s{t}") for t in range(PACK - 1)]
        for z in range(2):
            res_raw = keep.tile([P, 2, T], F32, name=f"stage{z + 1}")
            nc.sync.dma_start(res_raw[:], res_rows[:, 2 * z : 2 * z + 2, :])
            for t in range(2):
                if 2 * z + t < PACK - 1:
                    nc.gpsimd.tensor_scalar(res_s[2 * z + t][:], res_raw[:, t, :], RES_WEIGHT, 0.0, ALU.mult, ALU.add)
        res_last = res_raw[:, 1, :]
        nc.gpsimd.memset(q_win[1][:], 0.0)

        q_turned = keep.tile([P, PACK, PACK, P], F32, name="q_turned")
        spare = q_turned[:].rearrange("p t s m -> p (t s m)")
        p_slot = [keep.tile([P, J], F32, name=f"p_slot{t}")[:] if t != 1 else spare[:, 0:J] for t in range(PACK)]
        q_slot = [keep.tile([P, J], F32, name=f"q_slot{t}") for t in range(PACK)]

        def first_pass(acc, t, z):
            cols = slice(t * P, (t + 1) * P)
            nc.tensor.matmul_mx(
                out=acc[:],
                lhsT=wa_code[z][:, cols].bitcast(FP8X4),
                lhsT_scale=wa_scale[z][:, cols],
                rhs=g_word["a", z].bitcast(FP4X4),
                rhs_scale=g_scale[z][:, 0:J],
                start=(z == 0),
                stop=(z == PASSES - 1),
            )

        def first_expert(t):
            acc = psum_p.tile([P, J], F32, name="p_acc")
            for z in range(PASSES):
                first_pass(acc, t, z)
            nc.scalar.copy(p_slot[t], acc[:])

        def second_pass(acc, s, z):
            nc.tensor.matmul_mx(
                out=acc[:],
                lhsT=g_word["b", z][:, 2 * s * P : 2 * (s + 1) * P].bitcast(FP4X4),
                lhsT_scale=g_scale[z][:, J + s * P : J + (s + 1) * P],
                rhs=wb_word[:, z, :].bitcast(FP8X4),
                rhs_scale=wb_scale[:, z, :],
                start=(z == 0),
                stop=(z == PASSES - 1),
            )

        def turn_back(t):
            acc = psum.tile([P, J], F32, name="q_acc")
            for s in range(PACK):
                nc.tensor.transpose(acc[:, s * P : (s + 1) * P], q_turned[:, t, s, :], ident[:])
            return acc

        y = keep.tile([P, PACK, T], F32, name="y")
        y_code = keep.tile([P, T], U32, name="y_code", align_bytes=64)
        y_scale = keep.tile([P, T], U8, name="y_scale", align_bytes=64)
        code_rows = out_1[0].rearrange("p c r -> p (c r)").bitcast(I32)
        edges = [0, 256, 512, 768, 1024]
        chunks = [slice(a, b) for a, b in zip(edges, edges[1:])]
        weak, base = {}, {}
        turned = keep.tile([P, T], F32, name="turned")
        bank = T // 2

        def sum_on_tensor(terms, staging):
            for h in range(2):
                fwd = psum_qt.tile([P, bank], F32, name="qt_acc")
                for b in range(PACK):
                    cols = slice(h * bank + b * P, h * bank + (b + 1) * P)
                    for i, term in enumerate(terms):
                        nc.tensor.matmul(
                            fwd[:, b * P : (b + 1) * P], term[:, cols], ident[:],
                            is_transpose=True, start=(i == 0), stop=(i == len(terms) - 1),
                        )
                nc.scalar.copy(staging[:, h * bank : (h + 1) * bank], fwd[:])
            back = []
            for h in range(2):
                bk = psum_qt.tile([P, bank], F32, name="qt_acc")
                for b in range(PACK):
                    cols = slice(h * bank + b * P, h * bank + (b + 1) * P)
                    nc.tensor.transpose(bk[:, b * P : (b + 1) * P], staging[:, cols], ident[:])
                back.append(bk)
            return back

        def place_first(t):
            pg = p_win[t % 3]
            nc.vector.tensor_copy(pg[:].indirect(list_a[:]), p_slot[t])
            size = [spare[:, J : J + T], size_one[:], turned[:], y[:, 0, :]][t]
            nc.scalar.activation(size, pg[:], ACT.Abs)
            weak[t] = ring.tile([P, T], F32, name="weak")
            nc.scalar.activation(weak[t][:], size, ACT.Exp, scale=-1.0)
            if t in (1, 2):
                base[t] = ring.tile([P, T], F32, name="weak")
                nc.gpsimd.tensor_tensor(base[t][:], pg[:], res_s[t][:], ALU.add)

        def place_second(t):
            qg = q_win[t % 2]
            nc.vector.tensor_copy(qg[:].indirect(list_b[:]), q_slot[t][:])
            extra = keep.tile([P, T], F32, name="extra_first" if t == 0 else "extra")
            if t == 0:
                nc.gpsimd.tensor_tensor(extra[:], qg[:], weak[t][:], ALU.mult)
                back = sum_on_tensor([p_win[0][:], res_s[0][:], extra[:]], turned[:])
                for h in range(2):
                    nc.scalar.copy(y[:, t, h * bank : (h + 1) * bank], back[h][:])
                nc.sync.dma_start(out_rows[:, t, :], y[:, t, :])
            elif t < PACK - 1:
                nc.gpsimd.tensor_tensor(extra[:], qg[:], weak[t][:], ALU.mult)
                nc.gpsimd.tensor_tensor(y[:, t, :], base[t][:], extra[:], ALU.add)
                nc.sync.dma_start(out_rows[:, t, :], y[:, t, :])
            else:
                last_base = keep.tile([P, T], F32, name="last_base", tag=f"q_slot{t}")

                def product(c):
                    nc.vector.tensor_tensor(extra[:, chunks[c]], qg[:, chunks[c]], weak[t][:, chunks[c]], ALU.mult)

                product(0)
                for c, cols in enumerate(chunks):
                    nc.vector.scalar_tensor_tensor(
                        last_base[:, cols], res_last[:, cols], RES_WEIGHT, p_win[t % 3][:, cols], ALU.mult, ALU.add
                    )
                    if c + 1 < CHUNKS:
                        product(c + 1)
                    else:
                        quantize_out(0)
                    nc.vector.tensor_tensor(y[:, t, cols], last_base[:, cols], extra[:, cols], ALU.add)
                    nc.sync.dma_start(out_rows[:, t, cols], y[:, t, cols])
                    round_pair(c, 2)
                for c in range(1, CHUNKS):
                    quantize_out(c)

        def quantize_out(c):
            cols = chunks[c]
            nc.vector.quantize_mx(
                out=y_code[:, cols].bitcast(FP8X4),
                scales=y_scale[:, cols],
                in_=y_bf[c][:].rearrange("p c t -> p (c t)"),
            )
            nc.sync.dma_start(code_rows[:, cols], y_code[:, cols].bitcast(I32))

        size_one = keep.tile([P, T], F32, name="size_one")
        p_acc = psum_p.tile([P, J], F32, name="p_acc")
        qt_acc = [psum_qt.tile([P, N], F32, name="qt_acc") for s in range(PACK)]
        for z in range(PASSES):
            first_pass(p_acc, 0, z)
            for s in range(PACK):
                second_pass(qt_acc[s], s, z)
        nc.scalar.copy(p_slot[0], p_acc[:])

        def gate_and_deal(ts):
            for s in range(PACK):
                nc.scalar.activation(
                    q_turned[:, ts, s, :],
                    qt_acc[s][:].rearrange("p (m t) -> p t m", t=PACK)[:, ts, :],
                    ACT.Copy,
                    scale=gate[:, s : s + 1],
                )

        gate_and_deal(slice(0, 1))
        q_acc = {0: turn_back(0)}
        nc.scalar.copy(q_slot[0][:], q_acc[0][:])
        gate_and_deal(slice(1, PACK))
        first_expert(1)
        q_acc[1] = turn_back(1)
        q_acc[2] = turn_back(2)
        place_first(0)
        p_win.append(keep.tile([P, T], F32, name="p_win2", tag="p_slot0"))
        nc.gpsimd.memset(p_win[2][:], 0.0)
        nc.scalar.copy(q_slot[1][:], q_acc[1][:])
        first_expert(2)
        nc.scalar.copy(q_slot[2][:], q_acc[2][:])
        q_acc[3] = turn_back(3)
        first_expert(3)
        nc.scalar.copy(q_slot[3][:], q_acc[3][:])
        place_second(0)
        y_bf = [keep.tile([P, s.stop - s.start, PACK], BF16, name=f"y_bf{c}", align_bytes=64) for c, s in enumerate(chunks)]

        def round_pair(c, t0):
            cols = chunks[c]
            nc.scalar.copy(y_bf[c][:, :, t0 : t0 + 2], y[:, t0 : t0 + 2, cols].rearrange("p t c -> p c t"))

        for t in range(1, PACK):
            place_first(t)
            if t == 2:
                for c in range(CHUNKS):
                    round_pair(c, 0)
            place_second(t)
        for q in range(QUADS):
            eng = nc.sync if q % 2 == 0 else nc.scalar
            eng.dma_start(out_2[0, 4 * q : 4 * q + 4, :].bitcast(I32), y_scale[32 * q : 32 * q + 4, :].bitcast(I32))
